import numpy as np, ml_dtypes
CORES = [14,30,46,62,78,94,110,126,134,150,166,182,198,214,230,246]
N = 16
ROOT = 11
def setup_inputs(rng):
    return {"x": rng.standard_normal((N, 128, N * 8), dtype=np.float32).astype(ml_dtypes.bfloat16)}
def reference(x):
    return {"y": np.stack([x[ROOT][:, r * 8:(r + 1) * 8] for r in range(N)])}

@@ -1,0 +1,54 @@
+from concourse.bass import DstId, RemoteDMATransfer
+
+N = 16
+BLK = 8
+S = 4
+NSLAB = N // S
+ENG = 8 // NSLAB
+
+SCRATCH = {
+    "stage": ("dram", [NSLAB, 128, S * BLK], "bfloat16"),
+    "land": ("dram", [128, S * BLK], "bfloat16"),
+}
+SEMAPHORES = ["staged", "sent", "arrived", "stored"]
+
+
+def rank_program(g, core, T, topo):
+    rank = T.rank_of(core)
+    if rank is None:
+        return
+    root = T.root
+    w = S * BLK
+
+    if rank != root:
+        c = (rank % S) * BLK
+        g.sync.wait_ge(T.sem.arrived, ENG)
+        g.sync.dma_start(T.y[:, :], T.land[:, c:c + BLK]).then_inc(T.sem.stored, 16)
+        g.sync.wait_ge(T.sem.stored, 16)
+        return
+
+    for q in range(NSLAB):
+        eng = g.sync if q % 2 == 0 else g.scalar
+        eng.dma_start(T.stage[q], T.x[:, q * w:(q + 1) * w]).then_inc(T.sem.staged, 16)
+    g.wait_ge(T.sem.staged, 16 * NSLAB)
+
+    transfers = []
+    for q in range(NSLAB):
+        ids = []
+        for r in range(q * S, (q + 1) * S):
+            if r == root:
+                continue
+            rid, pid = topo.addr(T.cores[r], core)
+            ids.append(DstId(rid=rid, pnc=pid))
+        transfers.append(RemoteDMATransfer(
+            dst_ids=ids,
+            dma_engine_mask=((1 << ENG) - 1) << (q * ENG),
+            remote_sem=T.sem.arrived,
+            srcs=[T.stage[q]],
+            dsts=[T.land[:, :] for _ in ids],
+        ))
+    g.remote_dma_fused(transfers, local_sem=T.sem.sent)
+
+    g.sync.wait_ge(T.sem.sent, ENG * NSLAB)
+    g.sync.dma_start(T.y[:, :], T.x[:, root * BLK:(root + 1) * BLK]).then_inc(T.sem.stored, 16)
+    g.sync.wait_ge(T.sem.stored, 16)

@@ -4,13 +4,14 @@ N = 16
 BLK = 8
 S = 4
 NSLAB = N // S
-ENG = 8 // NSLAB
+PER = 2
+ENG = 8 // PER
 
 SCRATCH = {
     "stage": ("dram", [NSLAB, 128, S * BLK], "bfloat16"),
     "land": ("dram", [128, S * BLK], "bfloat16"),
 }
-SEMAPHORES = ["staged", "sent", "arrived", "stored"]
+SEMAPHORES = ["staged0", "staged1", "sent", "arrived", "stored"]
 
 
 def rank_program(g, core, T, topo):
@@ -29,25 +30,27 @@ def rank_program(g, core, T, topo):
 
     for q in range(NSLAB):
         eng = g.sync if q % 2 == 0 else g.scalar
-        eng.dma_start(T.stage[q], T.x[:, q * w:(q + 1) * w]).then_inc(T.sem.staged, 16)
-    g.wait_ge(T.sem.staged, 16 * NSLAB)
+        eng.dma_start(T.stage[q], T.x[:, q * w:(q + 1) * w]).then_inc(T.sem["staged%d" % (q // PER)], 16)
 
-    transfers = []
-    for q in range(NSLAB):
-        ids = []
-        for r in range(q * S, (q + 1) * S):
-            if r == root:
-                continue
-            rid, pid = topo.addr(T.cores[r], core)
-            ids.append(DstId(rid=rid, pnc=pid))
-        transfers.append(RemoteDMATransfer(
-            dst_ids=ids,
-            dma_engine_mask=((1 << ENG) - 1) << (q * ENG),
-            remote_sem=T.sem.arrived,
-            srcs=[T.stage[q]],
-            dsts=[T.land[:, :] for _ in ids],
-        ))
-    g.remote_dma_fused(transfers, local_sem=T.sem.sent)
+    for k in range(NSLAB // PER):
+        transfers = []
+        for j in range(PER):
+            q = k * PER + j
+            ids = []
+            for r in range(q * S, (q + 1) * S):
+                if r == root:
+                    continue
+                rid, pid = topo.addr(T.cores[r], core)
+                ids.append(DstId(rid=rid, pnc=pid))
+            transfers.append(RemoteDMATransfer(
+                dst_ids=ids,
+                dma_engine_mask=((1 << ENG) - 1) << (j * ENG),
+                remote_sem=T.sem.arrived,
+                srcs=[T.stage[q]],
+                dsts=[T.land[:, :] for _ in ids],
+            ))
+        g.wait_ge(T.sem["staged%d" % k], 16 * PER)
+        g.remote_dma_fused(transfers, local_sem=T.sem.sent)
 
     g.sync.wait_ge(T.sem.sent, ENG * NSLAB)
     g.sync.dma_start(T.y[:, :], T.x[:, root * BLK:(root + 1) * BLK]).then_inc(T.sem.stored, 16)

@@ -4,8 +4,8 @@ N = 16
 BLK = 8
 S = 4
 NSLAB = N // S
-PER = 2
-ENG = 8 // PER
+CALLS = ((0, 3), (1, 2))
+ENG = 4
 
 SCRATCH = {
     "stage": ("dram", [NSLAB, 128, S * BLK], "bfloat16"),
@@ -28,14 +28,14 @@ def rank_program(g, core, T, topo):
         g.sync.wait_ge(T.sem.stored, 16)
         return
 
-    for q in range(NSLAB):
-        eng = g.sync if q % 2 == 0 else g.scalar
-        eng.dma_start(T.stage[q], T.x[:, q * w:(q + 1) * w]).then_inc(T.sem["staged%d" % (q // PER)], 16)
+    for k, slabs in enumerate(CALLS):
+        for j, q in enumerate(slabs):
+            eng = g.sync if j == 0 else g.scalar
+            eng.dma_start(T.stage[q], T.x[:, q * w:(q + 1) * w]).then_inc(T.sem["staged%d" % k], 16)
 
-    for k in range(NSLAB // PER):
+    for k, slabs in enumerate(CALLS):
         transfers = []
-        for j in range(PER):
-            q = k * PER + j
+        for j, q in enumerate(slabs):
             ids = []
             for r in range(q * S, (q + 1) * S):
                 if r == root:
@@ -49,7 +49,7 @@ def rank_program(g, core, T, topo):
                 srcs=[T.stage[q]],
                 dsts=[T.land[:, :] for _ in ids],
             ))
-        g.wait_ge(T.sem["staged%d" % k], 16 * PER)
+        g.wait_ge(T.sem["staged%d" % k], 16 * len(slabs))
         g.remote_dma_fused(transfers, local_sem=T.sem.sent)
 
     g.sync.wait_ge(T.sem.sent, ENG * NSLAB)

from concourse.bass import DstId, RemoteDMATransfer

N = 16
BLK = 8
S = 4
NSLAB = N // S
CALLS = ((0, 3), (1, 2))
ENG = 4

SCRATCH = {
    "stage": ("dram", [NSLAB, 128, S * BLK], "bfloat16"),
    "land": ("dram", [128, S * BLK], "bfloat16"),
}
SEMAPHORES = ["staged0", "staged1", "sent", "arrived", "stored"]


def rank_program(g, core, T, topo):
    rank = T.rank_of(core)
    if rank is None:
        return
    root = T.root
    w = S * BLK

    if rank != root:
        c = (rank % S) * BLK
        g.sync.wait_ge(T.sem.arrived, ENG)
        g.sync.dma_start(T.y[:, :], T.land[:, c:c + BLK]).then_inc(T.sem.stored, 16)
        g.sync.wait_ge(T.sem.stored, 16)
        return

    for k, slabs in enumerate(CALLS):
        for j, q in enumerate(slabs):
            eng = g.sync if j == 0 else g.scalar
            eng.dma_start(T.stage[q], T.x[:, q * w:(q + 1) * w]).then_inc(T.sem["staged%d" % k], 16)

    for k, slabs in enumerate(CALLS):
        transfers = []
        for j, q in enumerate(slabs):
            ids = []
            for r in range(q * S, (q + 1) * S):
                if r == root:
                    continue
                rid, pid = topo.addr(T.cores[r], core)
                ids.append(DstId(rid=rid, pnc=pid))
            transfers.append(RemoteDMATransfer(
                dst_ids=ids,
                dma_engine_mask=((1 << ENG) - 1) << (j * ENG),
                remote_sem=T.sem.arrived,
                srcs=[T.stage[q]],
                dsts=[T.land[:, :] for _ in ids],
            ))
        g.wait_ge(T.sem["staged%d" % k], 16 * len(slabs))
        g.remote_dma_fused(transfers, local_sem=T.sem.sent)

    g.sync.wait_ge(T.sem.sent, ENG * NSLAB)
    g.sync.dma_start(T.y[:, :], T.x[:, root * BLK:(root + 1) * BLK]).then_inc(T.sem.stored, 16)
    g.sync.wait_ge(T.sem.stored, 16)
